import numpy as np
import ml_dtypes


def mxq(x, axis, fmt="e4m3"):
    dtype, down = {"e4m3": (ml_dtypes.float8_e4m3fn, 7), "e5m2": (ml_dtypes.float8_e5m2, 14)}[fmt]
    v = np.moveaxis(np.asarray(x, np.float32).astype(ml_dtypes.bfloat16).astype(np.float64), axis, -1)
    blocks = v.reshape(v.shape[:-1] + (-1, 32))
    amax = np.abs(blocks).max(-1, keepdims=True)
    byte = np.maximum(np.where(amax > 0, np.frexp(amax)[1] - 1 + 127, 0) - down, 1)
    scale = np.exp2(byte - 127.0)
    codes = (blocks / scale).astype(np.float32).astype(dtype).astype(np.float64)
    return np.moveaxis((codes * scale).reshape(v.shape), -1, axis)


WIDE = False


def mx_kscale(k):
    if not WIDE:
        return np.ones(k)
    levels = np.array([10, -10, 5, -5, 0])
    if k % 512:
        return np.exp2(np.random.permutation(np.resize(levels, k // 32))).repeat(32)
    a = np.empty((k // 512, 16))
    for p in range(k // 512):
        a[p, :8] = np.random.permutation(np.resize(levels, 8))
        for g in range(8):
            far = levels[np.abs(levels - a[p, g]) >= 10]
            a[p, g + 8] = far[np.random.randint(len(far))]
    return np.exp2(a.ravel()).repeat(32)


def f64(x):
    return np.asarray(x).astype(np.float64)


def striped(idx):
    return np.tile(idx.reshape(-1, 16).T, (8, 1)).astype(np.uint16)


def unstriped(offs):
    return offs[:16].T.reshape(-1).astype(np.int64)


E2M1 = np.array([0.0, 0.5, 1.0, 1.5, 2.0, 3.0, 4.0, 6.0, -0.0, -0.5, -1.0, -1.5, -2.0, -3.0, -4.0, -6.0])


def pack_weight(w, fmt):
    k, n = w.shape
    w = f64(np.asarray(w, np.float32).astype(ml_dtypes.bfloat16)).reshape(k // 32, 32, n)
    amax = np.abs(w).max(1)
    if fmt == "e4m3":
        byte = np.frexp(amax)[1] - 1 + 127 - 7
    else:
        mant, ex = np.frexp(amax / 6.0)
        byte = np.where(mant > 0.5, ex, ex - 1) + 127
    byte = np.clip(np.where(amax > 0, byte, 1), 1, 254)
    scaled = (w * np.exp2(127.0 - byte)[:, None, :]).reshape(k, n).astype(np.float32)
    by_word = np.ascontiguousarray(scaled.reshape(k // 512, 128, 4, n).transpose(0, 1, 3, 2))
    if fmt == "e4m3":
        words = by_word.astype(ml_dtypes.float8_e4m3fn).view(np.uint8)
    else:
        c = by_word.astype(ml_dtypes.float4_e2m1fn).view(np.uint8) & 0xF
        words = (c[..., 0::2] | (c[..., 1::2] << 4)).reshape(k // 512, 128, 2 * n)
    return np.ascontiguousarray(words), np.ascontiguousarray(byte.astype(np.uint8).reshape(k // 512, 16, n))


def unpack_weight(words, scales, fmt):
    g, _, n = scales.shape
    words = np.ascontiguousarray(words).reshape(g, 128, n, -1)
    if fmt == "e4m3":
        vals = words.view(ml_dtypes.float8_e4m3fn).astype(np.float64)
    else:
        nib = np.empty((g, 128, n, 4), np.uint8)
        nib[..., 0::2] = words & 0xF
        nib[..., 1::2] = words >> 4
        vals = E2M1[nib]
    vals = vals * np.repeat(np.exp2(scales.astype(np.float64) - 127.0), 8, axis=1)[..., None]
    return vals.transpose(0, 1, 3, 2).reshape(g * 512, n)


def relu2(v):
    return np.maximum(v, 0.0) ** 2


K, T, E, C, N = 1024, 768, 24, 128, 128
TOP = 4


def by_expert(wq, xq):
    return np.concatenate([wq[e].T @ xq[:, e * C:(e + 1) * C] for e in range(E)], axis=1)


def setup_inputs():
    n = np.random.standard_normal
    s = mx_kscale(K)[:, None]
    deal = np.repeat(np.arange(E), C).reshape(TOP, T)[:, np.random.permutation(T)]
    deal = np.take_along_axis(deal, np.argsort(np.random.rand(TOP, T), axis=0), axis=0)
    for _ in range(8):
        s_, t_ = np.random.permutation(T).reshape(2, -1); r = np.random.randint(TOP, size=T // 2); x, y = deal[r, s_].copy(), deal[r, t_].copy()
        ok = ~((deal[:, s_] == y).any(0) | (deal[:, t_] == x).any(0)); deal[r[ok], s_[ok]] = y[ok]; deal[r[ok], t_[ok]] = x[ok]
    order = np.lexsort((np.random.rand(TOP * T), deal.reshape(-1)))
    slot_token = order % T; pos = np.empty(TOP * T, np.int64); pos[order] = np.arange(TOP * T); pos = pos.reshape(TOP, T)
    g = np.random.uniform(0.5, 1.5, (TOP, T)); g = g / g.sum(0)
    x = pack_weight(n((K, T)) * s, "e4m3")
    return {
        "x_words": x[0],
        "x_scales": x[1],
        "w": (n((E, K, N)) / np.sqrt(K) / s[None]).astype(np.float32),
        "b": (0.3 * n((N, E))).astype(np.float32),
        "gate": np.stack([np.tile(r, (N, 1)) for r in g]).astype(np.float32),
        "offs": striped(slot_token),
        "pos1": striped(pos[0]),
        "pos2": striped(pos[1]),
        "pos3": striped(pos[2]),
        "pos4": striped(pos[3]),
    }


def reference(x_words, x_scales, w, b, gate, offs, pos1, pos2, pos3, pos4):
    idx = unstriped(offs)
    xq = unpack_weight(x_words, x_scales, "e4m3")[:, idx]
    y = by_expert(mxq(f64(w), 1, "e4m3"), xq)
    y = relu2(y + np.repeat(f64(b), C, axis=1))
    return sum(f64(gate[r]) * y[:, unstriped(p)] for r, p in enumerate((pos1, pos2, pos3, pos4)))

@@ -1,0 +1,233 @@
+from contextlib import ExitStack
+
+import concourse.mybir as mybir
+from concourse.masks import make_identity
+
+K, T, E, C, N = 1024, 768, 24, 128, 128
+TOP = 4
+FLOPS = 2 * K * N * E * C
+
+F32 = mybir.dt.float32
+BF16 = mybir.dt.bfloat16
+I32 = mybir.dt.int32
+U32 = mybir.dt.uint32
+U16 = mybir.dt.uint16
+U8 = mybir.dt.uint8
+FP8X4 = mybir.dt.float8_e4m3fn_x4
+ACT = mybir.ActivationFunctionType
+ALU = mybir.AluOpType
+
+P = 128
+PACK = 4
+PASSES = K // (P * PACK)
+SLABS = E * PASSES
+SLAB_BYTES = PACK * N * 4
+PAIR_BYTES = 2 * PASSES * SLAB_BYTES
+GROUP = 4
+GSLOTS = GROUP * C
+GROUPS = E // GROUP
+RUN = 4
+HALF = T // 2
+CHUNKS = HALF // P
+
+LOADS = [(0, 2), (2, 4)] + [(s, s + 4) for s in range(4, 44, 4)] + [(44, 46), (46, 47), (47, 48)]
+ON_VECTOR = [(10, 12), (18, 20), (26, 28), (34, 36), (46, 47), (47, 48)]
+
+
+def tile_moe_pkd_lin_relu2_kernel(
+    tc, x_words, x_scales, w, b, gate, offs, pos1, pos2, pos3, pos4, out
+):
+    nc = tc.nc
+    with ExitStack() as ctx:
+        lists = ctx.enter_context(tc.tile_pool(name="lists", bufs=1))
+        keep = ctx.enter_context(tc.tile_pool(name="keep", bufs=1))
+        placed = ctx.enter_context(tc.tile_pool(name="placed", bufs=1))
+        stage = ctx.enter_context(tc.tile_pool(name="stage", bufs=6))
+        psum = ctx.enter_context(tc.psum_pool(name="psum", bufs=1))
+
+        offs_sb = lists.tile([P, E * C // 16], U16, name="offs_sb")
+        pos_sb = [lists.tile([P, T // 16], U16, name="pos_sb%d" % r) for r in range(TOP)]
+        xw = [keep.tile([P, T], I32, name="xw%d" % o, align_bytes=64) for o in range(PASSES)]
+        xs = keep.tile([P, T], U8, name="xs", align_bytes=64)
+        bias = keep.tile([P, E], F32, name="bias")
+        ident = keep.tile([P, P], F32, name="ident")
+        gate_rows = keep.tile([P, P], F32, name="gate_rows")
+        gate_cols = keep.tile([P, (TOP - 1) * 2 * CHUNKS], F32, name="gate_cols")
+        gate_last = keep.tile([P, T], F32, name="gate_last")
+        y = keep.tile([P, E * C], F32, name="y")
+
+        nc.vector.memset(xs[:].bitcast(I32), 0)
+        nc.vector.memset(gate_rows[:], 0.0)
+        make_identity(nc, ident[:])
+
+        w_slabs = w.rearrange("e (o p j) n -> p (e o) (j n)", o=PASSES, j=PACK)
+        raw = {}
+
+        def load_w(lo, hi):
+            raw[lo] = placed.tile(
+                [P, hi - lo, PACK, N], F32, name="raw%d" % lo, offset=lo * SLAB_BYTES, align_bytes=64
+            )
+            nc.sync.dma_start(out=raw[lo][:].rearrange("p s j n -> p s (j n)"), in_=w_slabs[:, lo:hi, :])
+
+        def load_words(o):
+            nc.sync.dma_start(out=xw[o][:], in_=x_words[o].rearrange("p t r -> p (t r)").bitcast(I32))
+
+        nc.scalar.dma_start(
+            out=gate_rows[0 : (TOP - 1) * 2 * CHUNKS, :],
+            in_=gate[0 : TOP - 1, 0, :].rearrange("r (c i) -> r c i", i=P),
+        )
+        nc.sync.dma_start(offs_sb[:], offs)
+        load_words(0)
+        for q in range(4):
+            nc.sync.dma_start(
+                out=xs[:].bitcast(I32)[32 * q : 32 * q + 4 * PASSES, :],
+                in_=x_scales[:, 4 * q : 4 * q + 4, :].bitcast(I32),
+            )
+        load_w(*LOADS[0])
+        load_words(1)
+        load_w(*LOADS[1])
+        nc.sync.dma_start(out=bias[:], in_=b)
+        for piece in LOADS[2:]:
+            load_w(*piece)
+        for r, pos in enumerate((pos1, pos2, pos3, pos4)):
+            nc.sync.dma_start(pos_sb[r][:], pos)
+        nc.sync.dma_start(out=gate_last[:], in_=gate[TOP - 1])
+
+        turned_gate = psum.tile([P, P], F32, name="turned_gate", tag="bank0")
+        nc.tensor.transpose(turned_gate[:], gate_rows[:], ident[:])
+        nc.scalar.activation(gate_cols[:], turned_gate[:, 0 : (TOP - 1) * 2 * CHUNKS], ACT.Copy)
+
+        spare = SLABS * SLAB_BYTES
+        words = {}
+        scales = {}
+
+        def gather_words(g, offset):
+            words[g] = placed.tile([P, PASSES, GSLOTS], U32, name="words%d" % g, offset=offset, align_bytes=64)
+            cut = offs_sb[:, g * GSLOTS // 16 : (g + 1) * GSLOTS // 16]
+            return [(words[g][:, o, :], xw[o][:].bitcast(U32).indirect(cut)) for o in range(PASSES)]
+
+        def gather_scales(g, offset):
+            scales[g] = placed.tile([P, GSLOTS], U8, name="scales%d" % g, offset=offset, align_bytes=64)
+            cut = offs_sb[:, g * GSLOTS // 16 : (g + 1) * GSLOTS // 16]
+            return [(scales[g][:], xs[:].indirect(cut))]
+
+        first_w = gather_words(0, spare)
+        first_s = gather_scales(0, spare + PASSES * GSLOTS * 4)
+        for dst, src in (first_w[0], first_s[0], first_w[1]):
+            nc.vector.tensor_copy(dst, src)
+
+        codes = {}
+
+        def quantize(piece_lo, lo, hi, engine):
+            n = hi - lo
+            grouped = stage.tile([P, n * N * PACK], BF16, name="grouped", tag="grouped", align_bytes=64)
+            src = raw[piece_lo][:, lo - piece_lo : hi - piece_lo].rearrange("p s j (c i) -> p s c j i", i=RUN)
+            dst = grouped[:].rearrange("p (s c i j) -> p s c j i", s=n, i=RUN, j=PACK)
+            if engine == "vector":
+                nc.vector.tensor_copy(dst, src)
+            else:
+                nc.scalar.copy(dst, src)
+            wq = keep.tile([P, n * N], U32, name="wq%d" % lo, align_bytes=64)
+            ws = keep.tile([P, n * N], U8, name="ws%d" % lo, align_bytes=64)
+            nc.vector.quantize_mx(out=wq[:].bitcast(FP8X4), scales=ws[:], in_=grouped[:])
+            for s in range(lo, hi):
+                cols = slice((s - lo) * N, (s - lo + 1) * N)
+                codes[s] = (wq[:, cols], ws[:, cols])
+
+        def quantize_piece(lo, hi):
+            mine = [u for u in ON_VECTOR if lo <= u[0] and u[1] <= hi]
+            if mine:
+                vlo, vhi = mine[0]
+                if lo < vlo:
+                    quantize(lo, lo, vlo, "scalar")
+                quantize(lo, vlo, vhi, "vector")
+            else:
+                quantize(lo, lo, hi, "scalar")
+
+        sums = {}
+
+        def multiply(first, count, bank):
+            acc = psum.tile([P, count * C], F32, name="acc", tag="bank%d" % bank)
+            sums[first] = acc
+            for i in range(count):
+                e = first + i
+                g, place = divmod(e, GROUP)
+                cols = slice(place * C, (place + 1) * C)
+                for o in range(PASSES):
+                    wq, ws = codes[e * PASSES + o]
+                    nc.tensor.matmul_mx(
+                        out=acc[:, i * C : (i + 1) * C],
+                        lhsT=wq.bitcast(FP8X4),
+                        lhsT_scale=ws,
+                        rhs=words[g][:, o, cols].bitcast(FP8X4),
+                        rhs_scale=scales[g][4 * o : P, cols],
+                        start=(o == 0),
+                        stop=(o == PASSES - 1),
+                    )
+
+        def finish(first, count, offset):
+            rect = placed.tile([P, count * C], F32, name="rect%d" % first, offset=offset, align_bytes=64)
+            for i in range(count):
+                e = first + i
+                nc.scalar.activation(
+                    rect[:, i * C : (i + 1) * C], sums[first][:, i * C : (i + 1) * C], ACT.Relu, bias=bias[:, e : e + 1]
+                )
+            nc.scalar.activation(y[:, first * C : (first + count) * C], rect[:], ACT.Square)
+
+        pairs = E // 2
+        for k in range(pairs):
+            last = k == pairs - 1
+            for lo, hi in LOADS:
+                if 4 * k <= lo < 4 * k + 4:
+                    quantize_piece(lo, hi)
+                    if last and hi % PASSES == 0:
+                        e = hi // PASSES - 1
+                        multiply(e, 1, (k + e) % 8)
+                        if e % 2 == 0:
+                            finish(2 * (k - 1), 2, k * PAIR_BYTES + 1024)
+                        finish(e, 1, spare + 8192 + (e % 2) * 512)
+            g = k // 2 + 1
+            if g < GROUPS:
+                if k % 2 == 0:
+                    moves = gather_words(g, k * PAIR_BYTES + 4096)
+                else:
+                    moves = gather_scales(g, k * PAIR_BYTES)
+                for dst, src in moves:
+                    nc.vector.tensor_copy(dst, src)
+            if not last:
+                multiply(2 * k, 2, k % 8)
+                if k > 0:
+                    finish(2 * (k - 1), 2, k * PAIR_BYTES + 1024)
+
+        total = {}
+        step = 0
+        for h in range(2):
+            for c in range(CHUNKS):
+                total[h, c] = psum.tile([P, P], F32, name="total", tag="bank%d" % (h * CHUNKS + c))
+            for r in range(TOP - 1):
+                picked = keep.tile([P, HALF], F32, name="picked%d" % step)
+                cut = pos_sb[r][:, h * HALF // 16 : (h + 1) * HALF // 16]
+                nc.vector.tensor_copy(picked[:], y[:].indirect(cut))
+                turned = psum.tile([P, HALF], F32, name="turned", tag="bank%d" % (6 + step % 2))
+                for c in range(CHUNKS):
+                    nc.tensor.transpose(turned[:, c * P : (c + 1) * P], picked[:, c * P : (c + 1) * P], ident[:])
+                for c in range(CHUNKS):
+                    gated = keep.tile([P, P], F32, name="gated%d_%d" % (step, c))
+                    col = r * 2 * CHUNKS + h * CHUNKS + c
+                    nc.scalar.activation(
+                        gated[:], turned[:, c * P : (c + 1) * P], ACT.Copy, scale=gate_cols[:, col : col + 1]
+                    )
+                    nc.tensor.matmul(
+                        total[h, c][:], gated[:], ident[:], start=(r == 0), stop=(r == TOP - 2), is_transpose=True
+                    )
+                step = step + 1
+        for h in range(2):
+            tokens = slice(h * HALF, (h + 1) * HALF)
+            product = keep.tile([P, HALF], F32, name="product%d" % h)
+            cut = pos_sb[TOP - 1][:, h * HALF // 16 : (h + 1) * HALF // 16]
+            nc.vector.tensor_tensor(product[:], y[:].indirect(cut), gate_last[:, tokens], ALU.mult)
+            result = keep.tile([P, HALF], F32, name="result%d" % h)
+            for c in range(CHUNKS):
+                cols = slice(c * P, (c + 1) * P)
+                nc.vector.tensor_tensor(result[:, cols], total[h, c][:], product[:, cols], ALU.add)
+            nc.sync.dma_start(out=out[:, tokens], in_=result[:])

@@ -26,11 +26,11 @@ PAIR_BYTES = 2 * PASSES * SLAB_BYTES
 GROUP = 4
 GSLOTS = GROUP * C
 GROUPS = E // GROUP
-RUN = 4
+RUN = 2
 HALF = T // 2
 CHUNKS = HALF // P
 
-LOADS = [(0, 2), (2, 4)] + [(s, s + 4) for s in range(4, 44, 4)] + [(44, 46), (46, 47), (47, 48)]
+LOADS = [(s, s + 2) for s in range(0, 46, 2)] + [(46, 47), (47, 48)]
 ON_VECTOR = [(10, 12), (18, 20), (26, 28), (34, 36), (46, 47), (47, 48)]
 
 
@@ -56,9 +56,9 @@ def tile_moe_pkd_lin_relu2_kernel(
         gate_last = keep.tile([P, T], F32, name="gate_last")
         y = keep.tile([P, E * C], F32, name="y")
 
-        nc.vector.memset(xs[:].bitcast(I32), 0)
-        nc.vector.memset(gate_rows[:], 0.0)
+        nc.gpsimd.memset(xs[:].bitcast(I32), 0)
         make_identity(nc, ident[:])
+        nc.scalar.activation(gate_rows[:], ident[:], ACT.Copy, scale=0.0)
 
         w_slabs = w.rearrange("e (o p j) n -> p (e o) (j n)", o=PASSES, j=PACK)
         raw = {}
@@ -72,30 +72,29 @@ def tile_moe_pkd_lin_relu2_kernel(
         def load_words(o):
             nc.sync.dma_start(out=xw[o][:], in_=x_words[o].rearrange("p t r -> p (t r)").bitcast(I32))
 
-        nc.scalar.dma_start(
-            out=gate_rows[0 : (TOP - 1) * 2 * CHUNKS, :],
-            in_=gate[0 : TOP - 1, 0, :].rearrange("r (c i) -> r c i", i=P),
-        )
         nc.sync.dma_start(offs_sb[:], offs)
-        load_words(0)
         for q in range(4):
             nc.sync.dma_start(
                 out=xs[:].bitcast(I32)[32 * q : 32 * q + 4 * PASSES, :],
                 in_=x_scales[:, 4 * q : 4 * q + 4, :].bitcast(I32),
             )
+        load_words(0)
         load_w(*LOADS[0])
         load_words(1)
         load_w(*LOADS[1])
         nc.sync.dma_start(out=bias[:], in_=b)
-        for piece in LOADS[2:]:
+        for piece in LOADS[2:8]:
+            load_w(*piece)
+        nc.sync.dma_start(
+            out=gate_rows[0 : (TOP - 1) * 2 * CHUNKS, :],
+            in_=gate[0 : TOP - 1, 0, :].rearrange("r (c i) -> r c i", i=P),
+        )
+        for piece in LOADS[8:]:
             load_w(*piece)
         for r, pos in enumerate((pos1, pos2, pos3, pos4)):
             nc.sync.dma_start(pos_sb[r][:], pos)
         nc.sync.dma_start(out=gate_last[:], in_=gate[TOP - 1])
 
-        turned_gate = psum.tile([P, P], F32, name="turned_gate", tag="bank0")
-        nc.tensor.transpose(turned_gate[:], gate_rows[:], ident[:])
-        nc.scalar.activation(gate_cols[:], turned_gate[:, 0 : (TOP - 1) * 2 * CHUNKS], ACT.Copy)
 
         spare = SLABS * SLAB_BYTES
         words = {}
@@ -113,7 +112,7 @@ def tile_moe_pkd_lin_relu2_kernel(
 
         first_w = gather_words(0, spare)
         first_s = gather_scales(0, spare + PASSES * GSLOTS * 4)
-        for dst, src in (first_w[0], first_s[0], first_w[1]):
+        for dst, src in (first_s[0], first_w[0], first_w[1]):
             nc.vector.tensor_copy(dst, src)
 
         codes = {}
@@ -186,12 +185,16 @@ def tile_moe_pkd_lin_relu2_kernel(
                         if e % 2 == 0:
                             finish(2 * (k - 1), 2, k * PAIR_BYTES + 1024)
                         finish(e, 1, spare + 8192 + (e % 2) * 512)
+            if k == 6:
+                turned_gate = psum.tile([P, P], F32, name="turned_gate", tag="bank7")
+                nc.tensor.transpose(turned_gate[:], gate_rows[:], ident[:])
+                nc.scalar.activation(gate_cols[:], turned_gate[:, 0 : (TOP - 1) * 2 * CHUNKS], ACT.Copy)
             g = k // 2 + 1
             if g < GROUPS:
                 if k % 2 == 0:
                     moves = gather_words(g, k * PAIR_BYTES + 4096)
                 else:
-                    moves = gather_scales(g, k * PAIR_BYTES)
+                    moves = gather_scales(g, k * PAIR_BYTES + 4096)
                 for dst, src in moves:
                     nc.vector.tensor_copy(dst, src)
             if not last:

@@ -31,7 +31,7 @@ HALF = T // 2
 CHUNKS = HALF // P
 
 LOADS = [(s, s + 2) for s in range(0, 46, 2)] + [(46, 47), (47, 48)]
-ON_VECTOR = [(10, 12), (18, 20), (26, 28), (34, 36), (46, 47), (47, 48)]
+ON_VECTOR = [(10, 12), (18, 20), (26, 28), (34, 36), (38, 40), (42, 44), (46, 47), (47, 48)]
 
 
 def tile_moe_pkd_lin_relu2_kernel(

@@ -21,17 +21,27 @@ P = 128
 PACK = 4
 PASSES = K // (P * PACK)
 SLABS = E * PASSES
-SLAB_BYTES = PACK * N * 4
-PAIR_BYTES = 2 * PASSES * SLAB_BYTES
-GROUP = 4
-GSLOTS = GROUP * C
+EXPERT_BYTES = PASSES * PACK * N * 4
+BANKS = 8
+PER_COLUMN = 16
+
+GROUP = 6
+GROUP_SLOTS = GROUP * C
 GROUPS = E // GROUP
-RUN = 2
+WINDOW = 1024
+SORTS = PASSES + 1
+
+PAIRS = E // 2
 HALF = T // 2
 CHUNKS = HALF // P
+TURNED = TOP - 1
+GATE_ROWS = TURNED * T // P
+LAST_STORE = P
 
-LOADS = [(s, s + 2) for s in range(0, 46, 2)] + [(46, 47), (47, 48)]
-ON_VECTOR = [(10, 12), (18, 20), (26, 28), (34, 36), (38, 40), (42, 44), (46, 47), (47, 48)]
+LOADS = [(s, s + PASSES) for s in range(0, SLABS - PASSES, PASSES)] + [(SLABS - 2, SLABS - 1), (SLABS - 1, SLABS)]
+UNITS = LOADS[:2] + [(s, s + 2 * PASSES) for s in range(2 * PASSES, SLABS - 2 * PASSES, 2 * PASSES)] + LOADS[-3:]
+EXPERTS_ON_VECTOR = 3
+SQUARES_ON_SCALAR = 4
 
 
 def tile_moe_pkd_lin_relu2_kernel(
@@ -42,21 +52,22 @@ def tile_moe_pkd_lin_relu2_kernel(
         lists = ctx.enter_context(tc.tile_pool(name="lists", bufs=1))
         keep = ctx.enter_context(tc.tile_pool(name="keep", bufs=1))
         placed = ctx.enter_context(tc.tile_pool(name="placed", bufs=1))
-        stage = ctx.enter_context(tc.tile_pool(name="stage", bufs=6))
+        stage = ctx.enter_context(tc.tile_pool(name="stage", bufs=4))
         psum = ctx.enter_context(tc.psum_pool(name="psum", bufs=1))
 
-        offs_sb = lists.tile([P, E * C // 16], U16, name="offs_sb")
-        pos_sb = [lists.tile([P, T // 16], U16, name="pos_sb%d" % r) for r in range(TOP)]
-        xw = [keep.tile([P, T], I32, name="xw%d" % o, align_bytes=64) for o in range(PASSES)]
-        xs = keep.tile([P, T], U8, name="xs", align_bytes=64)
+        offs_sb = lists.tile([P, E * C // PER_COLUMN], U16, name="offs_sb")
+        pos_sb = [lists.tile([P, T // PER_COLUMN], U16, name="pos_sb%d" % r) for r in range(TOP)]
+        xw = keep.tile([P, (PASSES - 1) * T + WINDOW], I32, name="xw", align_bytes=64)
+        xs = keep.tile([P, WINDOW], U8, name="xs", align_bytes=64)
         bias = keep.tile([P, E], F32, name="bias")
         ident = keep.tile([P, P], F32, name="ident")
         gate_rows = keep.tile([P, P], F32, name="gate_rows")
-        gate_cols = keep.tile([P, (TOP - 1) * 2 * CHUNKS], F32, name="gate_cols")
+        gate_cols = keep.tile([P, GATE_ROWS], F32, name="gate_cols")
         gate_last = keep.tile([P, T], F32, name="gate_last")
         y = keep.tile([P, E * C], F32, name="y")
 
         nc.gpsimd.memset(xs[:].bitcast(I32), 0)
+        nc.gpsimd.memset(xw[:, PASSES * T :], 0)
         make_identity(nc, ident[:])
         nc.scalar.activation(gate_rows[:], ident[:], ACT.Copy, scale=0.0)
 
@@ -65,101 +76,83 @@ def tile_moe_pkd_lin_relu2_kernel(
 
         def load_w(lo, hi):
             raw[lo] = placed.tile(
-                [P, hi - lo, PACK, N], F32, name="raw%d" % lo, offset=lo * SLAB_BYTES, align_bytes=64
+                [P, hi - lo, PACK, N], F32, name="raw%d" % lo, offset=lo * EXPERT_BYTES // PASSES, align_bytes=64
             )
             nc.sync.dma_start(out=raw[lo][:].rearrange("p s j n -> p s (j n)"), in_=w_slabs[:, lo:hi, :])
-
-        def load_words(o):
-            nc.sync.dma_start(out=xw[o][:], in_=x_words[o].rearrange("p t r -> p (t r)").bitcast(I32))
 
         nc.sync.dma_start(offs_sb[:], offs)
         for q in range(4):
             nc.sync.dma_start(
-                out=xs[:].bitcast(I32)[32 * q : 32 * q + 4 * PASSES, :],
+                out=xs[:].bitcast(I32)[32 * q : 32 * q + 4 * PASSES, 0 : T // 4],
                 in_=x_scales[:, 4 * q : 4 * q + 4, :].bitcast(I32),
             )
-        load_words(0)
-        load_w(*LOADS[0])
-        load_words(1)
-        load_w(*LOADS[1])
+        nc.sync.dma_start(
+            out=xw[:, 0 : PASSES * T].rearrange("p (o t) -> p o t", o=PASSES),
+            in_=x_words.rearrange("o p t r -> p o (t r)").bitcast(I32),
+        )
+        for piece in LOADS[:2]:
+            load_w(*piece)
         nc.sync.dma_start(out=bias[:], in_=b)
         for piece in LOADS[2:8]:
             load_w(*piece)
         nc.sync.dma_start(
-            out=gate_rows[0 : (TOP - 1) * 2 * CHUNKS, :],
-            in_=gate[0 : TOP - 1, 0, :].rearrange("r (c i) -> r c i", i=P),
+            out=gate_rows[0:GATE_ROWS, :], in_=gate[0:TURNED, 0, :].rearrange("r (c i) -> r c i", i=P)
         )
         for piece in LOADS[8:]:
             load_w(*piece)
         for r, pos in enumerate((pos1, pos2, pos3, pos4)):
             nc.sync.dma_start(pos_sb[r][:], pos)
-        nc.sync.dma_start(out=gate_last[:], in_=gate[TOP - 1])
+        nc.sync.dma_start(out=gate_last[:], in_=gate[TURNED])
 
+        spare = E * EXPERT_BYTES
+        gathered = {}
 
-        spare = SLABS * SLAB_BYTES
-        words = {}
-        scales = {}
-
-        def gather_words(g, offset):
-            words[g] = placed.tile([P, PASSES, GSLOTS], U32, name="words%d" % g, offset=offset, align_bytes=64)
-            cut = offs_sb[:, g * GSLOTS // 16 : (g + 1) * GSLOTS // 16]
-            return [(words[g][:, o, :], xw[o][:].bitcast(U32).indirect(cut)) for o in range(PASSES)]
-
-        def gather_scales(g, offset):
-            scales[g] = placed.tile([P, GSLOTS], U8, name="scales%d" % g, offset=offset, align_bytes=64)
-            cut = offs_sb[:, g * GSLOTS // 16 : (g + 1) * GSLOTS // 16]
-            return [(scales[g][:], xs[:].indirect(cut))]
-
-        first_w = gather_words(0, spare)
-        first_s = gather_scales(0, spare + PASSES * GSLOTS * 4)
-        for dst, src in (first_s[0], first_w[0], first_w[1]):
-            nc.vector.tensor_copy(dst, src)
+        def gather(g, sort, offset):
+            cut = offs_sb[:, g * GROUP_SLOTS // PER_COLUMN : (g + 1) * GROUP_SLOTS // PER_COLUMN]
+            if sort == 0:
+                dtype, window = U8, xs[:]
+            else:
+                dtype, window = U32, xw[:].bitcast(U32)[:, (sort - 1) * T : (sort - 1) * T + WINDOW]
+            gathered[g, sort] = placed.tile(
+                [P, GROUP_SLOTS], dtype, name="gathered%d_%d" % (g, sort), offset=offset, align_bytes=64
+            )
+            nc.vector.tensor_copy(gathered[g, sort][:], window.indirect(cut))
 
         codes = {}
 
-        def quantize(piece_lo, lo, hi, engine):
-            n = hi - lo
-            grouped = stage.tile([P, n * N * PACK], BF16, name="grouped", tag="grouped", align_bytes=64)
-            src = raw[piece_lo][:, lo - piece_lo : hi - piece_lo].rearrange("p s j (c i) -> p s c j i", i=RUN)
-            dst = grouped[:].rearrange("p (s c i j) -> p s c j i", s=n, i=RUN, j=PACK)
-            if engine == "vector":
-                nc.vector.tensor_copy(dst, src)
-            else:
-                nc.scalar.copy(dst, src)
-            wq = keep.tile([P, n * N], U32, name="wq%d" % lo, align_bytes=64)
-            ws = keep.tile([P, n * N], U8, name="ws%d" % lo, align_bytes=64)
+        def quantize(lo, hi):
+            grouped = stage.tile([P, (hi - lo) * N * PACK], BF16, name="grouped", align_bytes=64)
+            for start, stop in LOADS:
+                if lo <= start < hi:
+                    src = raw[start][:].rearrange("p s j (c i) -> p s c j i", i=2)
+                    part = grouped[:, (start - lo) * N * PACK : (stop - lo) * N * PACK]
+                    dst = part.rearrange("p (s c i j) -> p s c j i", s=stop - start, i=2, j=PACK)
+                    if start // PASSES >= E - EXPERTS_ON_VECTOR:
+                        nc.vector.tensor_copy(dst, src)
+                    else:
+                        nc.scalar.copy(dst, src)
+            wq = keep.tile([P, (hi - lo) * N], U32, name="wq%d" % lo, align_bytes=64)
+            ws = keep.tile([P, (hi - lo) * N], U8, name="ws%d" % lo, align_bytes=64)
             nc.vector.quantize_mx(out=wq[:].bitcast(FP8X4), scales=ws[:], in_=grouped[:])
             for s in range(lo, hi):
                 cols = slice((s - lo) * N, (s - lo + 1) * N)
                 codes[s] = (wq[:, cols], ws[:, cols])
 
-        def quantize_piece(lo, hi):
-            mine = [u for u in ON_VECTOR if lo <= u[0] and u[1] <= hi]
-            if mine:
-                vlo, vhi = mine[0]
-                if lo < vlo:
-                    quantize(lo, lo, vlo, "scalar")
-                quantize(lo, vlo, vhi, "vector")
-            else:
-                quantize(lo, lo, hi, "scalar")
-
         sums = {}
 
-        def multiply(first, count, bank):
-            acc = psum.tile([P, count * C], F32, name="acc", tag="bank%d" % bank)
-            sums[first] = acc
+        def multiply(first, count):
+            sums[first] = psum.tile([P, count * C], F32, name="sums", tag="bank%d" % (len(sums) % BANKS))
             for i in range(count):
-                e = first + i
-                g, place = divmod(e, GROUP)
-                cols = slice(place * C, (place + 1) * C)
+                g, place = divmod(first + i, GROUP)
+                slots = slice(place * C, (place + 1) * C)
                 for o in range(PASSES):
-                    wq, ws = codes[e * PASSES + o]
+                    wq, ws = codes[(first + i) * PASSES + o]
                     nc.tensor.matmul_mx(
-                        out=acc[:, i * C : (i + 1) * C],
+                        out=sums[first][:, i * C : (i + 1) * C],
                         lhsT=wq.bitcast(FP8X4),
                         lhsT_scale=ws,
-                        rhs=words[g][:, o, cols].bitcast(FP8X4),
-                        rhs_scale=scales[g][4 * o : P, cols],
+                        rhs=gathered[g, 1 + o][:, slots].bitcast(FP8X4),
+                        rhs_scale=gathered[g, 0][4 * o : P, slots],
                         start=(o == 0),
                         stop=(o == PASSES - 1),
                     )
@@ -167,70 +160,74 @@ def tile_moe_pkd_lin_relu2_kernel(
         def finish(first, count, offset):
             rect = placed.tile([P, count * C], F32, name="rect%d" % first, offset=offset, align_bytes=64)
             for i in range(count):
+                cols = slice(i * C, (i + 1) * C)
                 e = first + i
-                nc.scalar.activation(
-                    rect[:, i * C : (i + 1) * C], sums[first][:, i * C : (i + 1) * C], ACT.Relu, bias=bias[:, e : e + 1]
-                )
-            nc.scalar.activation(y[:, first * C : (first + count) * C], rect[:], ACT.Square)
+                nc.scalar.activation(rect[:, cols], sums[first][:, cols], ACT.Relu, bias=bias[:, e : e + 1])
+            slots = slice(first * C, (first + count) * C)
+            if first >= E - SQUARES_ON_SCALAR:
+                nc.scalar.activation(y[:, slots], rect[:], ACT.Square)
+            else:
+                nc.gpsimd.tensor_tensor(y[:, slots], rect[:], rect[:], ALU.mult)
 
-        pairs = E // 2
-        for k in range(pairs):
-            last = k == pairs - 1
-            for lo, hi in LOADS:
-                if 4 * k <= lo < 4 * k + 4:
-                    quantize_piece(lo, hi)
-                    if last and hi % PASSES == 0:
-                        e = hi // PASSES - 1
-                        multiply(e, 1, (k + e) % 8)
-                        if e % 2 == 0:
-                            finish(2 * (k - 1), 2, k * PAIR_BYTES + 1024)
-                        finish(e, 1, spare + 8192 + (e % 2) * 512)
-            if k == 6:
-                turned_gate = psum.tile([P, P], F32, name="turned_gate", tag="bank7")
-                nc.tensor.transpose(turned_gate[:], gate_rows[:], ident[:])
-                nc.scalar.activation(gate_cols[:], turned_gate[:, 0 : (TOP - 1) * 2 * CHUNKS], ACT.Copy)
-            g = k // 2 + 1
+        for sort in range(SORTS):
+            gather(0, sort, spare + sort * EXPERT_BYTES)
+
+        for k in range(PAIRS - 1):
+            for lo, hi in UNITS:
+                if lo // (2 * PASSES) == k:
+                    quantize(lo, hi)
+            g, sort = divmod(k + SORTS, SORTS)
             if g < GROUPS:
-                if k % 2 == 0:
-                    moves = gather_words(g, k * PAIR_BYTES + 4096)
-                else:
-                    moves = gather_scales(g, k * PAIR_BYTES + 4096)
-                for dst, src in moves:
-                    nc.vector.tensor_copy(dst, src)
-            if not last:
-                multiply(2 * k, 2, k % 8)
-                if k > 0:
-                    finish(2 * (k - 1), 2, k * PAIR_BYTES + 1024)
+                gather(g, sort, (2 * k + 1) * EXPERT_BYTES)
+            if k == PAIRS // 2:
+                turned_gate = psum.tile([P, P], F32, name="turned_gate", tag="bank%d" % (BANKS - 1))
+                nc.tensor.transpose(turned_gate[:], gate_rows[:], ident[:])
+                nc.scalar.activation(gate_cols[:], turned_gate[:, 0:GATE_ROWS], ACT.Copy)
+            multiply(2 * k, 2)
+            if k > 0:
+                finish(2 * (k - 1), 2, 2 * k * EXPERT_BYTES)
 
-        total = {}
-        step = 0
+        quantize(*UNITS[-3])
+        multiply(E - 2, 1)
+        finish(E - 4, 2, (E - 2) * EXPERT_BYTES)
+        finish(E - 2, 1, spare + SORTS * EXPERT_BYTES)
+        quantize(*UNITS[-2])
+        quantize(*UNITS[-1])
+        multiply(E - 1, 1)
+        finish(E - 1, 1, spare + SORTS * EXPERT_BYTES + C * 4)
+
+        total = []
         for h in range(2):
-            for c in range(CHUNKS):
-                total[h, c] = psum.tile([P, P], F32, name="total", tag="bank%d" % (h * CHUNKS + c))
-            for r in range(TOP - 1):
+            gated = {}
+            for r in range(TURNED):
+                step = h * TURNED + r
                 picked = keep.tile([P, HALF], F32, name="picked%d" % step)
-                cut = pos_sb[r][:, h * HALF // 16 : (h + 1) * HALF // 16]
+                cut = pos_sb[r][:, h * HALF // PER_COLUMN : (h + 1) * HALF // PER_COLUMN]
                 nc.vector.tensor_copy(picked[:], y[:].indirect(cut))
-                turned = psum.tile([P, HALF], F32, name="turned", tag="bank%d" % (6 + step % 2))
+                turned = psum.tile([P, HALF], F32, name="turned", tag="bank%d" % (2 + step))
                 for c in range(CHUNKS):
                     nc.tensor.transpose(turned[:, c * P : (c + 1) * P], picked[:, c * P : (c + 1) * P], ident[:])
                 for c in range(CHUNKS):
-                    gated = keep.tile([P, P], F32, name="gated%d_%d" % (step, c))
-                    col = r * 2 * CHUNKS + h * CHUNKS + c
+                    gated[r, c] = keep.tile([P, P], F32, name="gated%d_%d" % (step, c))
+                    col = (2 * r + h) * CHUNKS + c
                     nc.scalar.activation(
-                        gated[:], turned[:, c * P : (c + 1) * P], ACT.Copy, scale=gate_cols[:, col : col + 1]
+                        gated[r, c][:], turned[:, c * P : (c + 1) * P], ACT.Copy, scale=gate_cols[:, col : col + 1]
                     )
-                    nc.tensor.matmul(
-                        total[h, c][:], gated[:], ident[:], start=(r == 0), stop=(r == TOP - 2), is_transpose=True
-                    )
-                step = step + 1
-        for h in range(2):
-            tokens = slice(h * HALF, (h + 1) * HALF)
-            product = keep.tile([P, HALF], F32, name="product%d" % h)
-            cut = pos_sb[TOP - 1][:, h * HALF // 16 : (h + 1) * HALF // 16]
-            nc.vector.tensor_tensor(product[:], y[:].indirect(cut), gate_last[:, tokens], ALU.mult)
-            result = keep.tile([P, HALF], F32, name="result%d" % h)
+            total.append(psum.tile([P, HALF], F32, name="total", tag="bank%d" % h))
             for c in range(CHUNKS):
-                cols = slice(c * P, (c + 1) * P)
-                nc.vector.tensor_tensor(result[:, cols], total[h, c][:], product[:, cols], ALU.add)
-            nc.sync.dma_start(out=out[:, tokens], in_=result[:])
+                for r in range(TURNED):
+                    nc.tensor.matmul(
+                        total[h][:, c * P : (c + 1) * P],
+                        gated[r, c][:],
+                        ident[:],
+                        start=(r == 0),
+                        stop=(r == TURNED - 1),
+                        is_transpose=True,
+                    )
+        product = keep.tile([P, T], F32, name="product")
+        nc.vector.tensor_tensor(product[:], y[:].indirect(pos_sb[TURNED][:]), gate_last[:], ALU.mult)
+        for lo, hi in ((0, HALF), (HALF, T - LAST_STORE), (T - LAST_STORE, T)):
+            h = lo // HALF
+            result = keep.tile([P, hi - lo], F32, name="result%d" % lo)
+            nc.vector.tensor_tensor(result[:], total[h][:, lo - h * HALF : hi - h * HALF], product[:, lo:hi], ALU.add)
+            nc.sync.dma_start(out=out[:, lo:hi], in_=result[:])

from contextlib import ExitStack

import concourse.mybir as mybir
from concourse.masks import make_identity

K, T, E, C, N = 1024, 768, 24, 128, 128
TOP = 4
FLOPS = 2 * K * N * E * C

F32 = mybir.dt.float32
BF16 = mybir.dt.bfloat16
I32 = mybir.dt.int32
U32 = mybir.dt.uint32
U16 = mybir.dt.uint16
U8 = mybir.dt.uint8
FP8X4 = mybir.dt.float8_e4m3fn_x4
ACT = mybir.ActivationFunctionType
ALU = mybir.AluOpType

P = 128
PACK = 4
PASSES = K // (P * PACK)
SLABS = E * PASSES
EXPERT_BYTES = PASSES * PACK * N * 4
BANKS = 8
PER_COLUMN = 16

GROUP = 6
GROUP_SLOTS = GROUP * C
GROUPS = E // GROUP
WINDOW = 1024
SORTS = PASSES + 1

PAIRS = E // 2
HALF = T // 2
CHUNKS = HALF // P
TURNED = TOP - 1
GATE_ROWS = TURNED * T // P
LAST_STORE = P

LOADS = [(s, s + PASSES) for s in range(0, SLABS - PASSES, PASSES)] + [(SLABS - 2, SLABS - 1), (SLABS - 1, SLABS)]
UNITS = LOADS[:2] + [(s, s + 2 * PASSES) for s in range(2 * PASSES, SLABS - 2 * PASSES, 2 * PASSES)] + LOADS[-3:]
EXPERTS_ON_VECTOR = 3
SQUARES_ON_SCALAR = 4


def tile_moe_pkd_lin_relu2_kernel(
    tc, x_words, x_scales, w, b, gate, offs, pos1, pos2, pos3, pos4, out
):
    nc = tc.nc
    with ExitStack() as ctx:
        lists = ctx.enter_context(tc.tile_pool(name="lists", bufs=1))
        keep = ctx.enter_context(tc.tile_pool(name="keep", bufs=1))
        placed = ctx.enter_context(tc.tile_pool(name="placed", bufs=1))
        stage = ctx.enter_context(tc.tile_pool(name="stage", bufs=4))
        psum = ctx.enter_context(tc.psum_pool(name="psum", bufs=1))

        offs_sb = lists.tile([P, E * C // PER_COLUMN], U16, name="offs_sb")
        pos_sb = [lists.tile([P, T // PER_COLUMN], U16, name="pos_sb%d" % r) for r in range(TOP)]
        xw = keep.tile([P, (PASSES - 1) * T + WINDOW], I32, name="xw", align_bytes=64)
        xs = keep.tile([P, WINDOW], U8, name="xs", align_bytes=64)
        bias = keep.tile([P, E], F32, name="bias")
        ident = keep.tile([P, P], F32, name="ident")
        gate_rows = keep.tile([P, P], F32, name="gate_rows")
        gate_cols = keep.tile([P, GATE_ROWS], F32, name="gate_cols")
        gate_last = keep.tile([P, T], F32, name="gate_last")
        y = keep.tile([P, E * C], F32, name="y")

        nc.gpsimd.memset(xs[:].bitcast(I32), 0)
        nc.gpsimd.memset(xw[:, PASSES * T :], 0)
        make_identity(nc, ident[:])
        nc.scalar.activation(gate_rows[:], ident[:], ACT.Copy, scale=0.0)

        w_slabs = w.rearrange("e (o p j) n -> p (e o) (j n)", o=PASSES, j=PACK)
        raw = {}

        def load_w(lo, hi):
            raw[lo] = placed.tile(
                [P, hi - lo, PACK, N], F32, name="raw%d" % lo, offset=lo * EXPERT_BYTES // PASSES, align_bytes=64
            )
            nc.sync.dma_start(out=raw[lo][:].rearrange("p s j n -> p s (j n)"), in_=w_slabs[:, lo:hi, :])

        nc.sync.dma_start(offs_sb[:], offs)
        for q in range(4):
            nc.sync.dma_start(
                out=xs[:].bitcast(I32)[32 * q : 32 * q + 4 * PASSES, 0 : T // 4],
                in_=x_scales[:, 4 * q : 4 * q + 4, :].bitcast(I32),
            )
        nc.sync.dma_start(
            out=xw[:, 0 : PASSES * T].rearrange("p (o t) -> p o t", o=PASSES),
            in_=x_words.rearrange("o p t r -> p o (t r)").bitcast(I32),
        )
        for piece in LOADS[:2]:
            load_w(*piece)
        nc.sync.dma_start(out=bias[:], in_=b)
        for piece in LOADS[2:8]:
            load_w(*piece)
        nc.sync.dma_start(
            out=gate_rows[0:GATE_ROWS, :], in_=gate[0:TURNED, 0, :].rearrange("r (c i) -> r c i", i=P)
        )
        for piece in LOADS[8:]:
            load_w(*piece)
        for r, pos in enumerate((pos1, pos2, pos3, pos4)):
            nc.sync.dma_start(pos_sb[r][:], pos)
        nc.sync.dma_start(out=gate_last[:], in_=gate[TURNED])

        spare = E * EXPERT_BYTES
        gathered = {}

        def gather(g, sort, offset):
            cut = offs_sb[:, g * GROUP_SLOTS // PER_COLUMN : (g + 1) * GROUP_SLOTS // PER_COLUMN]
            if sort == 0:
                dtype, window = U8, xs[:]
            else:
                dtype, window = U32, xw[:].bitcast(U32)[:, (sort - 1) * T : (sort - 1) * T + WINDOW]
            gathered[g, sort] = placed.tile(
                [P, GROUP_SLOTS], dtype, name="gathered%d_%d" % (g, sort), offset=offset, align_bytes=64
            )
            nc.vector.tensor_copy(gathered[g, sort][:], window.indirect(cut))

        codes = {}

        def quantize(lo, hi):
            grouped = stage.tile([P, (hi - lo) * N * PACK], BF16, name="grouped", align_bytes=64)
            for start, stop in LOADS:
                if lo <= start < hi:
                    src = raw[start][:].rearrange("p s j (c i) -> p s c j i", i=2)
                    part = grouped[:, (start - lo) * N * PACK : (stop - lo) * N * PACK]
                    dst = part.rearrange("p (s c i j) -> p s c j i", s=stop - start, i=2, j=PACK)
                    if start // PASSES >= E - EXPERTS_ON_VECTOR:
                        nc.vector.tensor_copy(dst, src)
                    else:
                        nc.scalar.copy(dst, src)
            wq = keep.tile([P, (hi - lo) * N], U32, name="wq%d" % lo, align_bytes=64)
            ws = keep.tile([P, (hi - lo) * N], U8, name="ws%d" % lo, align_bytes=64)
            nc.vector.quantize_mx(out=wq[:].bitcast(FP8X4), scales=ws[:], in_=grouped[:])
            for s in range(lo, hi):
                cols = slice((s - lo) * N, (s - lo + 1) * N)
                codes[s] = (wq[:, cols], ws[:, cols])

        sums = {}

        def multiply(first, count):
            sums[first] = psum.tile([P, count * C], F32, name="sums", tag="bank%d" % (len(sums) % BANKS))
            for i in range(count):
                g, place = divmod(first + i, GROUP)
                slots = slice(place * C, (place + 1) * C)
                for o in range(PASSES):
                    wq, ws = codes[(first + i) * PASSES + o]
                    nc.tensor.matmul_mx(
                        out=sums[first][:, i * C : (i + 1) * C],
                        lhsT=wq.bitcast(FP8X4),
                        lhsT_scale=ws,
                        rhs=gathered[g, 1 + o][:, slots].bitcast(FP8X4),
                        rhs_scale=gathered[g, 0][4 * o : P, slots],
                        start=(o == 0),
                        stop=(o == PASSES - 1),
                    )

        def finish(first, count, offset):
            rect = placed.tile([P, count * C], F32, name="rect%d" % first, offset=offset, align_bytes=64)
            for i in range(count):
                cols = slice(i * C, (i + 1) * C)
                e = first + i
                nc.scalar.activation(rect[:, cols], sums[first][:, cols], ACT.Relu, bias=bias[:, e : e + 1])
            slots = slice(first * C, (first + count) * C)
            if first >= E - SQUARES_ON_SCALAR:
                nc.scalar.activation(y[:, slots], rect[:], ACT.Square)
            else:
                nc.gpsimd.tensor_tensor(y[:, slots], rect[:], rect[:], ALU.mult)

        for sort in range(SORTS):
            gather(0, sort, spare + sort * EXPERT_BYTES)

        for k in range(PAIRS - 1):
            for lo, hi in UNITS:
                if lo // (2 * PASSES) == k:
                    quantize(lo, hi)
            g, sort = divmod(k + SORTS, SORTS)
            if g < GROUPS:
                gather(g, sort, (2 * k + 1) * EXPERT_BYTES)
            if k == PAIRS // 2:
                turned_gate = psum.tile([P, P], F32, name="turned_gate", tag="bank%d" % (BANKS - 1))
                nc.tensor.transpose(turned_gate[:], gate_rows[:], ident[:])
                nc.scalar.activation(gate_cols[:], turned_gate[:, 0:GATE_ROWS], ACT.Copy)
            multiply(2 * k, 2)
            if k > 0:
                finish(2 * (k - 1), 2, 2 * k * EXPERT_BYTES)

        quantize(*UNITS[-3])
        multiply(E - 2, 1)
        finish(E - 4, 2, (E - 2) * EXPERT_BYTES)
        finish(E - 2, 1, spare + SORTS * EXPERT_BYTES)
        quantize(*UNITS[-2])
        quantize(*UNITS[-1])
        multiply(E - 1, 1)
        finish(E - 1, 1, spare + SORTS * EXPERT_BYTES + C * 4)

        total = []
        for h in range(2):
            gated = {}
            for r in range(TURNED):
                step = h * TURNED + r
                picked = keep.tile([P, HALF], F32, name="picked%d" % step)
                cut = pos_sb[r][:, h * HALF // PER_COLUMN : (h + 1) * HALF // PER_COLUMN]
                nc.vector.tensor_copy(picked[:], y[:].indirect(cut))
                turned = psum.tile([P, HALF], F32, name="turned", tag="bank%d" % (2 + step))
                for c in range(CHUNKS):
                    nc.tensor.transpose(turned[:, c * P : (c + 1) * P], picked[:, c * P : (c + 1) * P], ident[:])
                for c in range(CHUNKS):
                    gated[r, c] = keep.tile([P, P], F32, name="gated%d_%d" % (step, c))
                    col = (2 * r + h) * CHUNKS + c
                    nc.scalar.activation(
                        gated[r, c][:], turned[:, c * P : (c + 1) * P], ACT.Copy, scale=gate_cols[:, col : col + 1]
                    )
            total.append(psum.tile([P, HALF], F32, name="total", tag="bank%d" % h))
            for c in range(CHUNKS):
                for r in range(TURNED):
                    nc.tensor.matmul(
                        total[h][:, c * P : (c + 1) * P],
                        gated[r, c][:],
                        ident[:],
                        start=(r == 0),
                        stop=(r == TURNED - 1),
                        is_transpose=True,
                    )
        product = keep.tile([P, T], F32, name="product")
        nc.vector.tensor_tensor(product[:], y[:].indirect(pos_sb[TURNED][:]), gate_last[:], ALU.mult)
        for lo, hi in ((0, HALF), (HALF, T - LAST_STORE), (T - LAST_STORE, T)):
            h = lo // HALF
            result = keep.tile([P, hi - lo], F32, name="result%d" % lo)
            nc.vector.tensor_tensor(result[:], total[h][:, lo - h * HALF : hi - h * HALF], product[:, lo:hi], ALU.add)
            nc.sync.dma_start(out=out[:, lo:hi], in_=result[:])
